import numpy as np
import ml_dtypes


def mxq(x, axis, fmt="e4m3"):
    dtype, down = {"e4m3": (ml_dtypes.float8_e4m3fn, 7), "e5m2": (ml_dtypes.float8_e5m2, 14)}[fmt]
    v = np.moveaxis(np.asarray(x, np.float32).astype(ml_dtypes.bfloat16).astype(np.float64), axis, -1)
    blocks = v.reshape(v.shape[:-1] + (-1, 32))
    amax = np.abs(blocks).max(-1, keepdims=True)
    byte = np.maximum(np.where(amax > 0, np.frexp(amax)[1] - 1 + 127, 0) - down, 1)
    scale = np.exp2(byte - 127.0)
    codes = (blocks / scale).astype(np.float32).astype(dtype).astype(np.float64)
    return np.moveaxis((codes * scale).reshape(v.shape), -1, axis)


WIDE = False


def mx_kscale(k):
    if not WIDE:
        return np.ones(k)
    levels = np.array([10, -10, 5, -5, 0])
    if k % 512:
        return np.exp2(np.random.permutation(np.resize(levels, k // 32))).repeat(32)
    a = np.empty((k // 512, 16))
    for p in range(k // 512):
        a[p, :8] = np.random.permutation(np.resize(levels, 8))
        for g in range(8):
            far = levels[np.abs(levels - a[p, g]) >= 10]
            a[p, g + 8] = far[np.random.randint(len(far))]
    return np.exp2(a.ravel()).repeat(32)


BF16 = ml_dtypes.bfloat16


def bf(x):
    return np.asarray(x, np.float32).astype(BF16)


def f64(x):
    return np.asarray(x).astype(np.float64)

def planes(Y):
    n, m = Y.shape
    b = f64(bf(Y)).reshape(n // 32, 32, m)
    amax = np.abs(b).max(1)
    byte = np.clip(np.where(amax > 0, np.frexp(amax)[1] - 1 + 127 - 7, 1), 1, 254)
    codes = (b * np.exp2(127.0 - byte)[:, None, :]).reshape(n, m).astype(np.float32).astype(ml_dtypes.float8_e4m3fn).view(np.uint8)
    words = codes.reshape(n // 512, 128, 4, m).transpose(0, 1, 3, 2)
    return np.ascontiguousarray(words), np.ascontiguousarray(byte.astype(np.uint8).reshape(n // 512, 16, m))


N, D, E, F, T, O = 1024, 512, 4, 512, 2, 512


def setup_inputs():
    kd, kf = mx_kscale(D), mx_kscale(F)
    return {
        "x": bf(np.random.standard_normal((N, D)) * kd),
        "we": bf(np.random.standard_normal((E, D, F)) / np.sqrt(D) / kd[None, :, None]),
        "be": bf(0.3 * np.random.standard_normal((E, F))),
        "wg": bf(1.5 * np.random.standard_normal((T, D, E)) / np.sqrt(D) / kd[None, :, None]),
        "s": bf(np.random.standard_normal((T, F)) * kf),
        "wt": bf(np.random.standard_normal((T, F, O)) / np.sqrt(F) / kf[None, :, None]),
        "c": bf(0.3 * np.random.standard_normal((T, O))),
    }


def expert_outputs(x, we, be):
    pre = (mxq(x, 1, "e4m3") @ mxq(we, 1, "e4m3")) + be[:, None, :]
    return np.maximum(pre, 0.0)


def task_gates(x, wg):
    q = np.stack([np.stack([np.sum(x * wg[t, :, e], axis=-1) for e in range(wg.shape[2])], axis=-1) for t in range(wg.shape[0])], axis=0)
    p = np.exp(q - q.max(-1, keepdims=True))
    return p / p.sum(-1, keepdims=True)


def mix_experts(gate, h):
    f = gate[:, :, 0, None] * h[None, 0]
    for e in range(1, h.shape[0]):
        f = f + gate[:, :, e, None] * h[None, e]
    return f


def core(x, we, be, wg, s, wt, c):
    x, we, be, wg, s, wt, c = f64(x), f64(we), f64(be), f64(wg), f64(s), f64(wt), f64(c)
    h = expert_outputs(x, we, be)
    gate = task_gates(x, wg)
    f = mix_experts(gate, h)
    fs = f * s[:, None, :]
    return (mxq(fs, 2, "e4m3") @ mxq(wt, 1, "e4m3")) + c[:, None, :]


def reference(x, we, be, wg, s, wt, c):
    R_out = core(x, we, be, wg, s, wt, c)
    words, scales = planes(np.moveaxis(R_out, 1, 0).reshape(1024, -1))
    return R_out, words, scales

@@ -1,0 +1,494 @@
+from contextlib import ExitStack
+
+import concourse.mybir as mybir
+from concourse.masks import make_identity
+
+N_TOK, D, E, F, T, O = 1024, 512, 4, 512, 2, 512
+FLOPS = 2 * N_TOK * D * E * F + 2 * N_TOK * D * T * E + 2 * T * N_TOK * F * O
+
+F32 = mybir.dt.float32
+BF16 = mybir.dt.bfloat16
+I32 = mybir.dt.int32
+U32 = mybir.dt.uint32
+U8 = mybir.dt.uint8
+FP8X4 = mybir.dt.float8_e4m3fn_x4
+ACT = mybir.ActivationFunctionType
+ALU = mybir.AluOpType
+AX = mybir.AxisListType
+
+P = 128
+PACK = 4
+GROUP = 32
+TILES = 8
+CHUNKS = 4
+CHUNK_TOK = 256
+PE_SLOTS = (0,)
+ACT_SLOTS = (3,)
+SPAN = 2
+MIX_LAG = 10
+TURN_LAG = 2
+SCALE_LAG = 3
+QUANT_LAG = 7
+TOWER_LAG = 9
+ADD_LAG = 10
+WT_AT = 11
+Y0_AT = 34
+Y_CUT = 192
+WARM = 6
+WT_ON_VECTOR = 4
+SM_AT = 5
+PWT_STEP = 1
+G1_AT = 0
+X_AT = (0, 2, 4, 6)
+G2_AT = 10
+PWT_AT = 0
+DIAG_AT = 0
+RUN = 1
+FIRST_TURN_ON_VECTOR = 2
+EXPERT_BANKS = 2
+TURN_BANKS = 2
+
+
+def tile_mmoetaskgatedexperttowers_x1_kernel(tc, x, we, be, wg, s, wt, c, out_0, out_1, out_2):
+    nc = tc.nc
+    with ExitStack() as ctx:
+        keep = ctx.enter_context(tc.tile_pool(name="keep", bufs=1))
+        work = ctx.enter_context(tc.tile_pool(name="work", bufs=2))
+        psum = ctx.enter_context(tc.psum_pool(name="psum", bufs=2))
+        ctx.enter_context(tc.manual_schedule())
+
+        ident = keep.tile([P, P], F32, align_bytes=64)
+        ident_bf = keep.tile([P, P], BF16, align_bytes=64)
+        spread = keep.tile([P, 4, E, GROUP], F32, align_bytes=64)
+        diag = keep.tile([P, GROUP], F32)
+        rows = keep.tile([P, F], BF16)
+        cols = keep.tile([P, PACK, 16], F32)
+        s_cols = keep.tile([P, T, PACK], F32)
+        wg_sb = keep.tile([P, T, PACK, E], BF16)
+        c_all = keep.tile([P, T, O], BF16)
+        x_raw = keep.tile([P, CHUNKS, 2, D], BF16, align_bytes=64)
+        x_k = keep.tile([P, N_TOK * PACK], BF16, align_bytes=64)
+        x_codes = keep.tile([P, N_TOK], U32, align_bytes=64)
+        x_scales = keep.tile([P, N_TOK], U8, align_bytes=64)
+        we_raw = keep.tile([P, E, PACK, F], BF16, align_bytes=64)
+        we_k = keep.tile([P, PACK, E * P, PACK], BF16, align_bytes=64)
+        we_codes = keep.tile([P, PACK, 4, P], U32, align_bytes=64)
+        we_scales = keep.tile([P, PACK, 4, P], U8, align_bytes=64)
+        wt_raw = keep.tile([P, T, PACK, O], BF16, align_bytes=64)
+        wt_k = keep.tile([P, T, O, PACK], BF16, align_bytes=64)
+        wt_codes = keep.tile([P, T, O], U32, align_bytes=64)
+        wt_scales = keep.tile([P, T, O], U8, align_bytes=64)
+        gate_col = keep.tile([P, TILES, 4, T], F32)
+        gate_diag = keep.tile([P, TILES * 4, T, GROUP], F32, align_bytes=64)
+        y = keep.tile([P, 2, PACK, T, O], F32, align_bytes=64)
+        y_codes = keep.tile([P, 2, T * O], U32, align_bytes=64)
+        y_scales = keep.tile([P, 2, T * O], U8, align_bytes=64)
+
+        h_feat, h_tok, mix_bank, fs_k, fs_q, tower, y_k, x_bank, turn_bank = {}, {}, {}, {}, {}, {}, {}, {}, {}
+        gate_state = {}
+
+        x_view = x.rearrange("(g m j) d -> m g j d", g=2, j=PACK)
+        out_view = out_0.rearrange("t (g m j) o -> m g j t o", g=2, j=PACK)
+        words_view = out_1.rearrange("g p m b -> p g (m b)").bitcast(I32)
+
+        def load_x(ch):
+            g, j0 = divmod(2 * ch, PACK)
+            nc.sync.dma_start(out=x_raw[:, ch], in_=x_view[:, g, j0 : j0 + 2, :])
+
+        def load_we(e):
+            nc.sync.dma_start(out=we_raw[:, e], in_=we[e].rearrange("(p j) f -> p j f", j=PACK))
+
+        def load_wt(t):
+            nc.sync.dma_start(out=wt_raw[:, t], in_=wt[t].rearrange("(p j) o -> p j o", j=PACK))
+
+        def turn_x(ch):
+            bank = psum.tile([P, 2, 2, P], F32, tag="tower", name="x_bank")
+            x_bank[ch] = bank
+            for tl in range(2):
+                words = x_raw[:, ch, tl, :].bitcast(F32).rearrange("p (w u) -> p u w", u=2)
+                for u in range(2):
+                    nc.tensor.transpose(bank[:, tl, u, :], words[:, u, :], ident[:])
+
+        def copy_x(ch):
+            dst = x_k[:, ch * 1024 : (ch + 1) * 1024].bitcast(F32).rearrange("p (t m u) -> p t m u", t=2, u=2)
+            nc.scalar.copy(out=dst, in_=x_bank[ch][:].rearrange("p t u m -> p t m u"))
+
+        def quantize_x(ch):
+            tok = slice(ch * CHUNK_TOK, (ch + 1) * CHUNK_TOK)
+            nc.vector.quantize_mx(
+                out=x_codes[:, tok].bitcast(FP8X4), scales=x_scales[:, tok], in_=x_k[:, ch * 1024 : (ch + 1) * 1024]
+            )
+
+        def logits(t0, t1):
+            n = t1 - t0
+            q = psum.tile([P, n, T, E], F32, tag="tower", name="logits")
+            x_cols = x_k[:].rearrange("p (n j) -> p j n", j=PACK)
+            for tl in range(n):
+                for j in range(PACK):
+                    nc.tensor.matmul(
+                        q[:, tl],
+                        lhsT=x_cols[:, j, (t0 + tl) * P : (t0 + tl + 1) * P],
+                        rhs=wg_sb[:, :, j, :],
+                        start=(j == 0),
+                        stop=(j == PACK - 1),
+                    )
+            top = work.tile([P, n * T], F32, name="top")
+            num = work.tile([P, n * T, E], F32, name="num")
+            den = work.tile([P, n * T], F32, name="den")
+            gate_state[t0] = (n, q[:].rearrange("p n t e -> p (n t) e"), top, num, den)
+
+        def softmax(t0, step):
+            n, q, top, num, den = gate_state[t0]
+            full = [P, n * T, E]
+            if step == 0:
+                nc.vector.tensor_reduce(out=top[:], in_=q, axis=AX.X, op=ALU.max)
+            elif step == 1:
+                nc.vector.tensor_tensor(out=num[:], in0=q, in1=top[:].unsqueeze(2).to_broadcast(full), op=ALU.subtract)
+            elif step == 2:
+                nc.scalar.activation(out=num[:], in_=num[:], func=ACT.Exp)
+            elif step == 3:
+                nc.vector.tensor_reduce(out=den[:], in_=num[:], axis=AX.X, op=ALU.add)
+            elif step == 4:
+                nc.vector.reciprocal(out=den[:], in_=den[:])
+            else:
+                nc.vector.tensor_tensor(out=num[:], in0=num[:], in1=den[:].unsqueeze(2).to_broadcast(full), op=ALU.mult)
+
+        def spread_gates(t0):
+            n, q, top, num, den = gate_state[t0]
+            rep = psum.tile([P, 4, n, T, E], F32, tag="tower", name="rep")
+            for a in range(4):
+                nc.tensor.matmul(
+                    rep[:, a].rearrange("p n t e -> p (n t e)"),
+                    lhsT=spread[:, a].rearrange("p e i -> p (e i)"),
+                    rhs=num[:].rearrange("p n e -> p (n e)"),
+                    start=True,
+                    stop=True,
+                )
+            gate_state[t0] = (n, rep)
+
+        def pick_gates(t0):
+            n, rep = gate_state[t0]
+            for e in range(E):
+                part = slice(e * GROUP, (e + 1) * GROUP)
+                nc.scalar.copy(
+                    out=gate_col[part, t0 : t0 + n].rearrange("p n a t -> p a n t"), in_=rep[part, :, :, :, e]
+                )
+
+        def diagonal_gates(tl):
+            full = [P, 4 * T, GROUP]
+            nc.gpsimd.tensor_tensor(
+                out=gate_diag[:, 4 * tl : 4 * tl + 4].rearrange("p a t i -> p (a t) i"),
+                in0=gate_col[:, tl].rearrange("p a t -> p (a t)").unsqueeze(2).to_broadcast(full),
+                in1=diag[:].unsqueeze(1).to_broadcast(full),
+                op=ALU.mult,
+            )
+
+        def interleave_we(e, j):
+            src = we_raw[:, e].rearrange("p d (c i j) -> p j c i d", c=4, j=PACK)[:, j]
+            order = "p (e c i) d -> p e c i d" if j in PE_SLOTS else "p (c e i) d -> p e c i d"
+            dst = we_k[:, j].rearrange(order, e=E, c=4)[:, e]
+            if j in ACT_SLOTS:
+                nc.scalar.copy(out=dst, in_=src)
+            else:
+                nc.vector.tensor_copy(out=dst, in_=src)
+
+        def quantize_we(j):
+            nc.vector.quantize_mx(
+                out=we_codes[:, j].rearrange("p r m -> p (r m)").bitcast(FP8X4),
+                scales=we_scales[:, j].rearrange("p r m -> p (r m)"),
+                in_=we_k[:, j].rearrange("p m d -> p (m d)"),
+            )
+
+        def interleave_wt(t, half):
+            o_cols = slice(half * 256, (half + 1) * 256)
+            src = wt_raw[:, t, :, o_cols].rearrange("p d o -> p o d")
+            if 2 * t + half < WT_ON_VECTOR:
+                nc.vector.tensor_copy(out=wt_k[:, t, o_cols, :], in_=src)
+            else:
+                nc.scalar.copy(out=wt_k[:, t, o_cols, :], in_=src)
+
+        def quantize_wt(t):
+            nc.vector.quantize_mx(
+                out=wt_codes[:, t].bitcast(FP8X4),
+                scales=wt_scales[:, t],
+                in_=wt_k[:, t].rearrange("p o d -> p (o d)"),
+            )
+
+        def experts(u):
+            ch, k = divmod(u, 4 * SPAN)
+            j, part = divmod(k, SPAN)
+            count = 4 // SPAN
+            tok = slice(ch * SPAN * P, (ch + 1) * SPAN * P)
+            bank = psum.tile([P, count, SPAN * P], F32, tag="expert", name="expert_bank", bufs=EXPERT_BANKS)
+            for i in range(count):
+                r = part * count + i
+                nc.tensor.matmul_mx(
+                    out=bank[:, i],
+                    lhsT=we_codes[:, j, r].bitcast(FP8X4),
+                    lhsT_scale=we_scales[:, j, r],
+                    rhs=x_codes[:, tok].bitcast(FP8X4),
+                    rhs_scale=x_scales[:, tok],
+                    start=True,
+                    stop=True,
+                )
+            if part == 0:
+                h_feat[ch, j] = work.tile([P, 4 * SPAN, 4, GROUP], F32, name="h_feat", bufs=4, align_bytes=64)
+            for i in range(count):
+                r = part * count + i
+                col = r if j in PE_SLOTS else 8 + r
+                nc.scalar.activation(
+                    out=h_feat[ch, j][:, :, r, :],
+                    in_=bank[:, i].rearrange("p (q i) -> p q i", i=GROUP),
+                    func=ACT.Relu,
+                    bias=cols[:, j, col : col + 1],
+                )
+
+        def feat(tl, j):
+            a0 = 4 * (tl % SPAN)
+            return h_feat[tl // SPAN, j][:, a0 : a0 + 4]
+
+        def token_tile(tl, j):
+            h_tok[tl, j] = work.tile([P, 4, P], F32, name="h_tok", bufs=16, align_bytes=64)
+            return h_tok[tl, j]
+
+        def turn_pe(tl, j):
+            bank = psum.tile([P, 4, P], F32, tag="turn", name="turn_bank", bufs=TURN_BANKS)
+            turn_bank[tl, j] = bank
+            for a in range(4):
+                nc.tensor.transpose(bank[:, a], feat(tl, j)[:, a].rearrange("p r i -> p (r i)"), ident[:])
+
+        def copy_turned(tl, j):
+            if tl < FIRST_TURN_ON_VECTOR:
+                nc.vector.tensor_copy(out=token_tile(tl, j)[:], in_=turn_bank[tl, j][:])
+            else:
+                nc.scalar.copy(out=token_tile(tl, j)[:], in_=turn_bank[tl, j][:])
+
+        def turn_dve(tl, j):
+            nc.vector.transpose(
+                out=token_tile(tl, j)[:].rearrange("p q m -> p (q m)"),
+                in_=feat(tl, j).rearrange("p q r i -> p (q r i)"),
+            )
+
+        def finished(u):
+            if not 0 <= u < 32 or u % SPAN != SPAN - 1:
+                return []
+            ch, k = divmod(u, 4 * SPAN)
+            return [(ch * SPAN + i, k // SPAN) for i in range(SPAN)]
+
+        def mix(q):
+            b, a = divmod(q, 2)
+            if a == 0:
+                mix_bank[b] = psum.tile([P, PACK, T, 2, GROUP], F32, tag="mix", name="mix_bank")
+            for j in range(PACK):
+                nc.tensor.matmul(
+                    mix_bank[b][:, j, :, a, :],
+                    lhsT=h_tok[q // 4, j][:, q % 4],
+                    rhs=gate_diag[:, q],
+                    start=True,
+                    stop=True,
+                )
+
+        def scale_mix(b):
+            tl, half = divmod(b, 2)
+            if half == 0:
+                fs_k[tl] = work.tile([P, T, P, PACK], BF16, name="fs_k", bufs=2, align_bytes=64)
+            nc.vector.tensor_tensor(
+                out=fs_k[tl][:, :, 64 * half : 64 * half + 64, :],
+                in0=mix_bank[b][:].rearrange("p j t a i -> p t (a i) j"),
+                in1=s_cols[:].unsqueeze(2).to_broadcast([P, T, 64, PACK]),
+                op=ALU.mult,
+            )
+
+        def quantize_fs(tl):
+            codes = work.tile([P, T, P], U32, name="fs_codes", bufs=2, align_bytes=64)
+            scales = work.tile([P, T, P], U8, name="fs_scales", bufs=2, align_bytes=64)
+            fs_q[tl] = (codes, scales)
+            nc.vector.quantize_mx(
+                out=codes[:].rearrange("p t m -> p (t m)").bitcast(FP8X4),
+                scales=scales[:].rearrange("p t m -> p (t m)"),
+                in_=fs_k[tl][:].rearrange("p t m j -> p (t m j)"),
+            )
+
+        def towers(tl):
+            codes, scales = fs_q[tl]
+            for t in range(T):
+                bank = psum.tile([P, O], F32, tag="tower", name="tower_bank")
+                tower[tl, t] = bank
+                nc.tensor.matmul_mx(
+                    out=bank[:],
+                    lhsT=codes[:, t].bitcast(FP8X4),
+                    lhsT_scale=scales[:, t],
+                    rhs=wt_codes[:, t].bitcast(FP8X4),
+                    rhs_scale=wt_scales[:, t],
+                    start=True,
+                    stop=True,
+                )
+
+        def add_c(tl, t):
+            g, jj = divmod(tl, PACK)
+            nc.vector.tensor_tensor(out=y[:, g, jj, t], in0=tower[tl, t][:], in1=c_all[:, t], op=ALU.add)
+
+        def store_y(tl, t):
+            g, jj = divmod(tl, PACK)
+            nc.sync.dma_start(out=out_view[:, g, jj, t], in_=y[:, g, jj, t])
+
+        def interleave_y(g, t, o0, o1, on_vector):
+            if (g, t) not in y_k:
+                y_k[g, t] = work.tile([P, O, PACK], BF16, name="y_k", bufs=2, align_bytes=64)
+            src = y[:, g, :, t, o0:o1].rearrange("p j o -> p o j")
+            if on_vector:
+                nc.vector.tensor_copy(out=y_k[g, t][:, o0:o1], in_=src)
+            else:
+                nc.scalar.copy(out=y_k[g, t][:, o0:o1], in_=src)
+
+        def quantize_y(g, t):
+            m_cols = slice(t * O, (t + 1) * O)
+            nc.vector.quantize_mx(
+                out=y_codes[:, g, m_cols].bitcast(FP8X4),
+                scales=y_scales[:, g, m_cols],
+                in_=y_k[g, t][:].rearrange("p o j -> p (o j)"),
+            )
+            nc.sync.dma_start(out=words_view[:, g, m_cols], in_=y_codes[:, g, m_cols].bitcast(I32))
+
+        def store_scales(g):
+            for quad in range(4):
+                eng = nc.scalar if g == 1 and quad % 2 else nc.sync
+                eng.dma_start(
+                    out=out_2[g, 4 * quad : 4 * quad + 4, :].bitcast(I32),
+                    in_=y_scales[32 * quad : 32 * quad + 4, g].bitcast(I32),
+                )
+
+        nc.vector.memset(rows[:], 0.0)
+        load_x(0)
+        nc.sync.dma_start(out=wg_sb[:].rearrange("p t j e -> p t (j e)"), in_=wg.rearrange("t (p j) e -> p t (j e)", j=PACK))
+        nc.sync.dma_start(out=rows[0:4, :], in_=be)
+        nc.sync.dma_start(out=rows[4:6, :], in_=s)
+        nc.sync.dma_start(out=rows[8:12, :].rearrange("c (e f) -> c e f", e=E), in_=be.rearrange("e (c f) -> c e f", c=4))
+        for e in range(E):
+            load_we(e)
+        for ch in range(1, CHUNKS):
+            load_x(ch)
+        for t in range(T):
+            load_wt(t)
+        nc.sync.dma_start(
+            out=c_all[:].rearrange("p t o -> p (t o)"), in_=c.rearrange("t o -> (t o)").partition_broadcast(P)
+        )
+        make_identity(nc, ident[:])
+        nc.vector.tensor_copy(out=ident_bf[:], in_=ident[:])
+        nc.vector.tensor_reduce(out=diag[:], in_=ident[:].rearrange("p (a i) -> p i a", a=4), axis=AX.X, op=ALU.add)
+        nc.scalar.activation(
+            out=spread[:],
+            in_=ident[:].rearrange("p (a i) -> p a i", a=4).unsqueeze(2).to_broadcast([P, 4, E, GROUP]),
+            func=ACT.Copy,
+        )
+
+        turn_x(0)
+        copy_x(0)
+        col_bank = psum.tile([P, PACK, P], BF16, tag="turn", name="col_bank", bufs=TURN_BANKS)
+        for j in range(PACK):
+            nc.tensor.transpose(col_bank[:, j], rows[:].rearrange("p (m j) -> p j m", j=PACK)[:, j], ident_bf[:])
+
+        def warm():
+            bank = psum.tile([P, CHUNK_TOK], F32, tag="mix", name="warm_bank")
+            for i in range(WARM):
+                nc.tensor.matmul_mx(
+                    out=bank[:],
+                    lhsT=x_codes[:, :P].bitcast(FP8X4),
+                    lhsT_scale=x_scales[:, :P],
+                    rhs=x_codes[:, :CHUNK_TOK].bitcast(FP8X4),
+                    rhs_scale=x_scales[:, :CHUNK_TOK],
+                    start=True,
+                    stop=True,
+                )
+
+        logits(0, 2)
+        for e in range(E):
+            for j in range(PACK):
+                interleave_we(e, j)
+                step = 3 * e + j - SM_AT
+                if j < 3 and 0 <= step < 6:
+                    softmax(0, step)
+                if e == 3 and j > 0:
+                    quantize_we(j - 1)
+            if e == 1:
+                quantize_x(0)
+                nc.scalar.copy(out=cols[:], in_=col_bank[:, :, 0:16])
+                nc.scalar.copy(out=s_cols[:], in_=col_bank[:, :, 4:6].rearrange("p j t -> p t j"))
+                warm()
+        quantize_we(3)
+
+        for n in range(56):
+            if n < 32 and n % RUN == 0:
+                for u in range(n, n + RUN):
+                    experts(u)
+            if n == G1_AT:
+                spread_gates(0)
+            if n == G1_AT + 1:
+                pick_gates(0)
+                diagonal_gates(0)
+                diagonal_gates(1)
+            for ch in range(1, CHUNKS):
+                if n == X_AT[ch] - 1:
+                    turn_x(ch)
+                if n == X_AT[ch]:
+                    copy_x(ch)
+                if n == X_AT[ch] + 1:
+                    quantize_x(ch)
+            if n == X_AT[3] + 1:
+                logits(2, TILES)
+            for step in range(6):
+                if n == G2_AT + (0, 0, 1, 1, 2, 2)[step]:
+                    softmax(2, step)
+            if n == G2_AT + 3:
+                spread_gates(2)
+                pick_gates(2)
+            if 2 <= n - G2_AT - 1 < TILES:
+                diagonal_gates(n - G2_AT - 1)
+            if 0 <= n - PWT_AT < 4 * PWT_STEP and (n - PWT_AT) % PWT_STEP == 0:
+                interleave_wt(*divmod((n - PWT_AT) // PWT_STEP, 2))
+            tl, k = divmod(n - MIX_LAG - TOWER_LAG, 4)
+            if 0 <= tl < TILES and k == 0:
+                towers(tl)
+            q = n - MIX_LAG
+            if 0 <= q < 32 and q % RUN == 0:
+                for i in range(RUN):
+                    mix(q + i)
+            for back in range(SPAN):
+                for tl, j in finished(n - TURN_LAG - back)[back : back + 1]:
+                    if j in PE_SLOTS:
+                        turn_pe(tl, j)
+                for tl, j in finished(n - TURN_LAG - 1 - back)[back : back + 1]:
+                    if j in PE_SLOTS:
+                        copy_turned(tl, j)
+            if n in (WT_AT, WT_AT + 2):
+                quantize_wt((n - WT_AT) // 2)
+            b, k = divmod(n - MIX_LAG - SCALE_LAG, 2)
+            if 0 <= b < 16 and k == 0:
+                scale_mix(b)
+            for back in range(SPAN):
+                for tl, j in finished(n - TURN_LAG - back)[back : back + 1]:
+                    if j not in PE_SLOTS:
+                        turn_dve(tl, j)
+            tl, k = divmod(n - MIX_LAG - QUANT_LAG, 4)
+            if 0 <= tl < TILES and k == 0:
+                quantize_fs(tl)
+            tl, k = divmod(n - MIX_LAG - ADD_LAG, 4)
+            if 0 <= tl < TILES and k < T:
+                add_c(tl, k)
+                store_y(tl, k)
+            piece = n - Y0_AT
+            if 0 <= piece < 4:
+                interleave_y(0, piece // 2, 256 * (piece % 2), 256 * (piece % 2 + 1), on_vector=False)
+            if n in (Y0_AT + 3, Y0_AT + 5):
+                quantize_y(0, (n - Y0_AT - 3) // 2)
+            if n == Y0_AT + 5:
+                store_scales(0)
+            t = n - (MIX_LAG + ADD_LAG + 28)
+            if 0 <= t < T:
+                interleave_y(1, t, 0, Y_CUT, on_vector=False)
+            if t == 1:
+                interleave_y(1, 0, Y_CUT, O, on_vector=True)
+                interleave_y(1, 1, Y_CUT, O, on_vector=True)
+                quantize_y(1, 0)
+                quantize_y(1, 1)
+                store_scales(1)

@@ -18,35 +18,37 @@ AX = mybir.AxisListType
 
 P = 128
 PACK = 4
-GROUP = 32
 TILES = 8
 CHUNKS = 4
-CHUNK_TOK = 256
-PE_SLOTS = (0,)
-ACT_SLOTS = (3,)
-SPAN = 2
-MIX_LAG = 10
-TURN_LAG = 2
-SCALE_LAG = 3
-QUANT_LAG = 7
-TOWER_LAG = 9
-ADD_LAG = 10
-WT_AT = 11
-Y0_AT = 34
-Y_CUT = 192
-WARM = 6
-WT_ON_VECTOR = 4
-SM_AT = 5
-PWT_STEP = 1
-G1_AT = 0
+WE_CUT = 3
+WE_CUT0 = 4
+POOL_ADDS = ()
+EARLY = 2
+BIAS_LAG = 1
+GATE_LAG = 2
+FIRST_SUM = 9
+SUM_STEP = 1
+SUM_AT = 9
+SCALE_LAG = 1
+QUANT_LAG = 1
+TOWER_LAG = 1
+ADD_LAG = 1
 X_AT = (0, 2, 4, 6)
-G2_AT = 10
-PWT_AT = 0
-DIAG_AT = 0
-RUN = 1
-FIRST_TURN_ON_VECTOR = 2
-EXPERT_BANKS = 2
-TURN_BANKS = 2
+G2_AT = 8
+WT_AT = 4
+WTQ_AT = 9
+Y0_AT = 28
+Y0Q = 6
+Y_CUT0 = 256
+TM_FROM = 8
+LEAD = 0
+IL_SHIFT = 0
+Y_CUT = 192
+DVE_GATES = ()
+EXPERT_BANKS = 3
+ZB_BUFS = 8
+U_BUFS = 22
+WARM = 0
 
 
 def tile_mmoetaskgatedexperttowers_x1_kernel(tc, x, we, be, wg, s, wt, c, out_0, out_1, out_2):
@@ -59,33 +61,29 @@ def tile_mmoetaskgatedexperttowers_x1_kernel(tc, x, we, be, wg, s, wt, c, out_0,
 
         ident = keep.tile([P, P], F32, align_bytes=64)
         ident_bf = keep.tile([P, P], BF16, align_bytes=64)
-        spread = keep.tile([P, 4, E, GROUP], F32, align_bytes=64)
-        diag = keep.tile([P, GROUP], F32)
         rows = keep.tile([P, F], BF16)
-        cols = keep.tile([P, PACK, 16], F32)
         s_cols = keep.tile([P, T, PACK], F32)
         wg_sb = keep.tile([P, T, PACK, E], BF16)
-        c_all = keep.tile([P, T, O], BF16)
+        be_all = keep.tile([P, E, F], BF16, align_bytes=64)
+        c_all = keep.tile([P, T, O], BF16, align_bytes=64)
         x_raw = keep.tile([P, CHUNKS, 2, D], BF16, align_bytes=64)
         x_k = keep.tile([P, N_TOK * PACK], BF16, align_bytes=64)
         x_codes = keep.tile([P, N_TOK], U32, align_bytes=64)
         x_scales = keep.tile([P, N_TOK], U8, align_bytes=64)
         we_raw = keep.tile([P, E, PACK, F], BF16, align_bytes=64)
-        we_k = keep.tile([P, PACK, E * P, PACK], BF16, align_bytes=64)
-        we_codes = keep.tile([P, PACK, 4, P], U32, align_bytes=64)
-        we_scales = keep.tile([P, PACK, 4, P], U8, align_bytes=64)
+        we_k = keep.tile([P, E, PACK, P, PACK], BF16, align_bytes=64)
+        we_codes = keep.tile([P, E, F], U32, align_bytes=64)
+        we_scales = keep.tile([P, E, F], U8, align_bytes=64)
         wt_raw = keep.tile([P, T, PACK, O], BF16, align_bytes=64)
         wt_k = keep.tile([P, T, O, PACK], BF16, align_bytes=64)
         wt_codes = keep.tile([P, T, O], U32, align_bytes=64)
         wt_scales = keep.tile([P, T, O], U8, align_bytes=64)
-        gate_col = keep.tile([P, TILES, 4, T], F32)
-        gate_diag = keep.tile([P, TILES * 4, T, GROUP], F32, align_bytes=64)
+        gate = keep.tile([P, TILES * T, E], F32)
         y = keep.tile([P, 2, PACK, T, O], F32, align_bytes=64)
         y_codes = keep.tile([P, 2, T * O], U32, align_bytes=64)
         y_scales = keep.tile([P, 2, T * O], U8, align_bytes=64)
 
-        h_feat, h_tok, mix_bank, fs_k, fs_q, tower, y_k, x_bank, turn_bank = {}, {}, {}, {}, {}, {}, {}, {}, {}
-        gate_state = {}
+        expert_bank, pre, gated, mix_bank, fs_k, fs_q, tower, y_k, x_bank, gate_state = ({} for i in range(10))
 
         x_view = x.rearrange("(g m j) d -> m g j d", g=2, j=PACK)
         out_view = out_0.rearrange("t (g m j) o -> m g j t o", g=2, j=PACK)
@@ -102,7 +100,7 @@ def tile_mmoetaskgatedexperttowers_x1_kernel(tc, x, we, be, wg, s, wt, c, out_0,
             nc.sync.dma_start(out=wt_raw[:, t], in_=wt[t].rearrange("(p j) o -> p j o", j=PACK))
 
         def turn_x(ch):
-            bank = psum.tile([P, 2, 2, P], F32, tag="tower", name="x_bank")
+            bank = psum.tile([P, 2, 2, P], F32, tag="spare", name="x_bank", bufs=1)
             x_bank[ch] = bank
             for tl in range(2):
                 words = x_raw[:, ch, tl, :].bitcast(F32).rearrange("p (w u) -> p u w", u=2)
@@ -114,7 +112,7 @@ def tile_mmoetaskgatedexperttowers_x1_kernel(tc, x, we, be, wg, s, wt, c, out_0,
             nc.scalar.copy(out=dst, in_=x_bank[ch][:].rearrange("p t u m -> p t m u"))
 
         def quantize_x(ch):
-            tok = slice(ch * CHUNK_TOK, (ch + 1) * CHUNK_TOK)
+            tok = slice(ch * 2 * P, (ch + 1) * 2 * P)
             nc.vector.quantize_mx(
                 out=x_codes[:, tok].bitcast(FP8X4), scales=x_scales[:, tok], in_=x_k[:, ch * 1024 : (ch + 1) * 1024]
             )
@@ -133,79 +131,59 @@ def tile_mmoetaskgatedexperttowers_x1_kernel(tc, x, we, be, wg, s, wt, c, out_0,
                         stop=(j == PACK - 1),
                     )
             top = work.tile([P, n * T], F32, name="top")
-            num = work.tile([P, n * T, E], F32, name="num")
             den = work.tile([P, n * T], F32, name="den")
-            gate_state[t0] = (n, q[:].rearrange("p n t e -> p (n t) e"), top, num, den)
+            gate_state[t0] = (n, q[:].rearrange("p n t e -> p (n t) e"), top, den)
 
         def softmax(t0, step):
-            n, q, top, num, den = gate_state[t0]
+            n, q, top, den = gate_state[t0]
+            num = gate[:, t0 * T : (t0 + n) * T]
             full = [P, n * T, E]
             if step == 0:
                 nc.vector.tensor_reduce(out=top[:], in_=q, axis=AX.X, op=ALU.max)
             elif step == 1:
-                nc.vector.tensor_tensor(out=num[:], in0=q, in1=top[:].unsqueeze(2).to_broadcast(full), op=ALU.subtract)
+                nc.vector.tensor_tensor(out=num, in0=q, in1=top[:].unsqueeze(2).to_broadcast(full), op=ALU.subtract)
             elif step == 2:
-                nc.scalar.activation(out=num[:], in_=num[:], func=ACT.Exp)
+                nc.scalar.activation(out=num, in_=num, func=ACT.Exp)
             elif step == 3:
-                nc.vector.tensor_reduce(out=den[:], in_=num[:], axis=AX.X, op=ALU.add)
+                nc.vector.tensor_reduce(out=den[:], in_=num, axis=AX.X, op=ALU.add)
             elif step == 4:
                 nc.vector.reciprocal(out=den[:], in_=den[:])
             else:
-                nc.vector.tensor_tensor(out=num[:], in0=num[:], in1=den[:].unsqueeze(2).to_broadcast(full), op=ALU.mult)
+                nc.vector.tensor_tensor(out=num, in0=num, in1=den[:].unsqueeze(2).to_broadcast(full), op=ALU.mult)
 
-        def spread_gates(t0):
-            n, q, top, num, den = gate_state[t0]
-            rep = psum.tile([P, 4, n, T, E], F32, tag="tower", name="rep")
-            for a in range(4):
+        def spread_bias(half):
+            bank = psum.tile([P, 2, F], BF16, tag="mix", name="bias_bank")
+            for i in range(2):
+                e = 2 * half + i
                 nc.tensor.matmul(
-                    rep[:, a].rearrange("p n t e -> p (n t e)"),
-                    lhsT=spread[:, a].rearrange("p e i -> p (e i)"),
-                    rhs=num[:].rearrange("p n e -> p (n e)"),
+                    bank[:, i].rearrange("p (j m) -> p j m", j=PACK),
+                    lhsT=ident_bf[:, e : e + 1].to_broadcast([P, P]),
+                    rhs=rows[:].rearrange("p (m j) -> p j m", j=PACK),
                     start=True,
                     stop=True,
                 )
-            gate_state[t0] = (n, rep)
-
-        def pick_gates(t0):
-            n, rep = gate_state[t0]
-            for e in range(E):
-                part = slice(e * GROUP, (e + 1) * GROUP)
-                nc.scalar.copy(
-                    out=gate_col[part, t0 : t0 + n].rearrange("p n a t -> p a n t"), in_=rep[part, :, :, :, e]
-                )
-
-        def diagonal_gates(tl):
-            full = [P, 4 * T, GROUP]
-            nc.gpsimd.tensor_tensor(
-                out=gate_diag[:, 4 * tl : 4 * tl + 4].rearrange("p a t i -> p (a t) i"),
-                in0=gate_col[:, tl].rearrange("p a t -> p (a t)").unsqueeze(2).to_broadcast(full),
-                in1=diag[:].unsqueeze(1).to_broadcast(full),
-                op=ALU.mult,
-            )
+            nc.scalar.copy(out=be_all[:, 2 * half : 2 * half + 2], in_=bank[:])
 
         def interleave_we(e, j):
-            src = we_raw[:, e].rearrange("p d (c i j) -> p j c i d", c=4, j=PACK)[:, j]
-            order = "p (e c i) d -> p e c i d" if j in PE_SLOTS else "p (c e i) d -> p e c i d"
-            dst = we_k[:, j].rearrange(order, e=E, c=4)[:, e]
-            if j in ACT_SLOTS:
-                nc.scalar.copy(out=dst, in_=src)
+            src = we_raw[:, e].rearrange("p d (m j) -> p j m d", j=PACK)[:, j]
+            if j >= (WE_CUT if e > 0 else WE_CUT0):
+                nc.scalar.copy(out=we_k[:, e, j], in_=src)
             else:
-                nc.vector.tensor_copy(out=dst, in_=src)
+                nc.vector.tensor_copy(out=we_k[:, e, j], in_=src)
 
-        def quantize_we(j):
+        def quantize_we(e):
             nc.vector.quantize_mx(
-                out=we_codes[:, j].rearrange("p r m -> p (r m)").bitcast(FP8X4),
-                scales=we_scales[:, j].rearrange("p r m -> p (r m)"),
-                in_=we_k[:, j].rearrange("p m d -> p (m d)"),
+                out=we_codes[:, e].bitcast(FP8X4),
+                scales=we_scales[:, e],
+                in_=we_k[:, e].rearrange("p j m d -> p (j m d)"),
             )
 
-        def interleave_wt(t, half):
-            o_cols = slice(half * 256, (half + 1) * 256)
-            src = wt_raw[:, t, :, o_cols].rearrange("p d o -> p o d")
-            if 2 * t + half < WT_ON_VECTOR:
-                nc.vector.tensor_copy(out=wt_k[:, t, o_cols, :], in_=src)
-            else:
-                nc.scalar.copy(out=wt_k[:, t, o_cols, :], in_=src)
+        def copy_on_pool(dst, src):
+            nc.gpsimd.tensor_scalar(out=dst, in0=src, scalar1=1.0, scalar2=0.0, op0=ALU.mult, op1=ALU.add)
+
+        def interleave_wt(t, part):
+            o_cols = slice(part * P, (part + 1) * P)
+            copy_on_pool(wt_k[:, t, o_cols, :], wt_raw[:, t, :, o_cols].rearrange("p d o -> p o d"))
 
         def quantize_wt(t):
             nc.vector.quantize_mx(
@@ -214,132 +192,100 @@ def tile_mmoetaskgatedexperttowers_x1_kernel(tc, x, we, be, wg, s, wt, c, out_0,
                 in_=wt_k[:, t].rearrange("p o d -> p (o d)"),
             )
 
-        def experts(u):
-            ch, k = divmod(u, 4 * SPAN)
-            j, part = divmod(k, SPAN)
-            count = 4 // SPAN
-            tok = slice(ch * SPAN * P, (ch + 1) * SPAN * P)
-            bank = psum.tile([P, count, SPAN * P], F32, tag="expert", name="expert_bank", bufs=EXPERT_BANKS)
-            for i in range(count):
-                r = part * count + i
-                nc.tensor.matmul_mx(
-                    out=bank[:, i],
-                    lhsT=we_codes[:, j, r].bitcast(FP8X4),
-                    lhsT_scale=we_scales[:, j, r],
-                    rhs=x_codes[:, tok].bitcast(FP8X4),
-                    rhs_scale=x_scales[:, tok],
-                    start=True,
-                    stop=True,
-                )
-            if part == 0:
-                h_feat[ch, j] = work.tile([P, 4 * SPAN, 4, GROUP], F32, name="h_feat", bufs=4, align_bytes=64)
-            for i in range(count):
-                r = part * count + i
-                col = r if j in PE_SLOTS else 8 + r
-                nc.scalar.activation(
-                    out=h_feat[ch, j][:, :, r, :],
-                    in_=bank[:, i].rearrange("p (q i) -> p q i", i=GROUP),
-                    func=ACT.Relu,
-                    bias=cols[:, j, col : col + 1],
-                )
-
-        def feat(tl, j):
-            a0 = 4 * (tl % SPAN)
-            return h_feat[tl // SPAN, j][:, a0 : a0 + 4]
-
-        def token_tile(tl, j):
-            h_tok[tl, j] = work.tile([P, 4, P], F32, name="h_tok", bufs=16, align_bytes=64)
-            return h_tok[tl, j]
-
-        def turn_pe(tl, j):
-            bank = psum.tile([P, 4, P], F32, tag="turn", name="turn_bank", bufs=TURN_BANKS)
-            turn_bank[tl, j] = bank
-            for a in range(4):
-                nc.tensor.transpose(bank[:, a], feat(tl, j)[:, a].rearrange("p r i -> p (r i)"), ident[:])
-
-        def copy_turned(tl, j):
-            if tl < FIRST_TURN_ON_VECTOR:
-                nc.vector.tensor_copy(out=token_tile(tl, j)[:], in_=turn_bank[tl, j][:])
-            else:
-                nc.scalar.copy(out=token_tile(tl, j)[:], in_=turn_bank[tl, j][:])
-
-        def turn_dve(tl, j):
-            nc.vector.transpose(
-                out=token_tile(tl, j)[:].rearrange("p q m -> p (q m)"),
-                in_=feat(tl, j).rearrange("p q r i -> p (q r i)"),
+        def expert(tl, e):
+            tok = slice(tl * P, (tl + 1) * P)
+            bank = psum.tile([P, F], F32, tag="expert", name="expert_bank", bufs=EXPERT_BANKS)
+            expert_bank[tl, e] = bank
+            nc.tensor.matmul_mx(
+                out=bank[:],
+                lhsT=x_codes[:, tok].bitcast(FP8X4),
+                lhsT_scale=x_scales[:, tok],
+                rhs=we_codes[:, e].bitcast(FP8X4),
+                rhs_scale=we_scales[:, e],
+                start=True,
+                stop=True,
             )
 
-        def finished(u):
-            if not 0 <= u < 32 or u % SPAN != SPAN - 1:
-                return []
-            ch, k = divmod(u, 4 * SPAN)
-            return [(ch * SPAN + i, k // SPAN) for i in range(SPAN)]
+        def add_bias(tl, e):
+            pre[tl, e] = work.tile([P, F], F32, name="pre", bufs=ZB_BUFS, align_bytes=64)
+            nc.vector.tensor_tensor(out=pre[tl, e][:], in0=expert_bank[tl, e][:], in1=be_all[:, e], op=ALU.add)
 
-        def mix(q):
-            b, a = divmod(q, 2)
-            if a == 0:
-                mix_bank[b] = psum.tile([P, PACK, T, 2, GROUP], F32, tag="mix", name="mix_bank")
+        def apply_gate(tl, e, t):
+            gated[tl, e, t] = work.tile([P, PACK, P], F32, name="gated", bufs=U_BUFS, align_bytes=64)
+            dst = gated[tl, e, t][:].rearrange("p j m -> p (j m)")
+            g = gate[:, tl * T + t, e : e + 1]
+            if (e, t) in DVE_GATES:
+                nc.vector.tensor_scalar(out=dst, in0=pre[tl, e][:], scalar1=g, scalar2=0.0, op0=ALU.mult, op1=ALU.max)
+            else:
+                nc.scalar.activation(out=dst, in_=pre[tl, e][:], func=ACT.Relu, scale=g)
+
+        def sum_experts(tl, t):
+            bank = psum.tile([P, PACK, P], F32, tag="mix", name="mix_bank")
+            mix_bank[tl, t] = bank
             for j in range(PACK):
-                nc.tensor.matmul(
-                    mix_bank[b][:, j, :, a, :],
-                    lhsT=h_tok[q // 4, j][:, q % 4],
-                    rhs=gate_diag[:, q],
-                    start=True,
-                    stop=True,
-                )
+                for e in range(E):
+                    nc.tensor.matmul(
+                        bank[:, j],
+                        lhsT=gated[tl, e, t][:, j],
+                        rhs=ident[:],
+                        start=(e == 0),
+                        stop=(e == E - 1),
+                        is_transpose=True,
+                    )
 
-        def scale_mix(b):
-            tl, half = divmod(b, 2)
-            if half == 0:
+        def scale_mix(tl, t):
+            if t == 0:
                 fs_k[tl] = work.tile([P, T, P, PACK], BF16, name="fs_k", bufs=2, align_bytes=64)
             nc.vector.tensor_tensor(
-                out=fs_k[tl][:, :, 64 * half : 64 * half + 64, :],
-                in0=mix_bank[b][:].rearrange("p j t a i -> p t (a i) j"),
-                in1=s_cols[:].unsqueeze(2).to_broadcast([P, T, 64, PACK]),
+                out=fs_k[tl][:, t],
+                in0=mix_bank[tl, t][:].rearrange("p j n -> p n j"),
+                in1=s_cols[:, t].unsqueeze(1).to_broadcast([P, P, PACK]),
                 op=ALU.mult,
             )
 
-        def quantize_fs(tl):
-            codes = work.tile([P, T, P], U32, name="fs_codes", bufs=2, align_bytes=64)
-            scales = work.tile([P, T, P], U8, name="fs_scales", bufs=2, align_bytes=64)
-            fs_q[tl] = (codes, scales)
+        def quantize_fs(tl, t):
+            codes = work.tile([P, P], U32, name="fs_codes", bufs=3, align_bytes=64)
+            scales = work.tile([P, P], U8, name="fs_scales", bufs=3, align_bytes=64)
+            fs_q[tl, t] = (codes, scales)
             nc.vector.quantize_mx(
-                out=codes[:].rearrange("p t m -> p (t m)").bitcast(FP8X4),
-                scales=scales[:].rearrange("p t m -> p (t m)"),
-                in_=fs_k[tl][:].rearrange("p t m j -> p (t m j)"),
+                out=codes[:].bitcast(FP8X4), scales=scales[:], in_=fs_k[tl][:, t].rearrange("p m j -> p (m j)")
             )
 
-        def towers(tl):
-            codes, scales = fs_q[tl]
-            for t in range(T):
-                bank = psum.tile([P, O], F32, tag="tower", name="tower_bank")
-                tower[tl, t] = bank
-                nc.tensor.matmul_mx(
-                    out=bank[:],
-                    lhsT=codes[:, t].bitcast(FP8X4),
-                    lhsT_scale=scales[:, t],
-                    rhs=wt_codes[:, t].bitcast(FP8X4),
-                    rhs_scale=wt_scales[:, t],
-                    start=True,
-                    stop=True,
-                )
+        def towers(tl, t):
+            codes, scales = fs_q[tl, t]
+            bank = psum.tile([P, O], F32, tag="tower", name="tower_bank")
+            tower[tl, t] = bank
+            nc.tensor.matmul_mx(
+                out=bank[:],
+                lhsT=codes[:].bitcast(FP8X4),
+                lhsT_scale=scales[:],
+                rhs=wt_codes[:, t].bitcast(FP8X4),
+                rhs_scale=wt_scales[:, t],
+                start=True,
+                stop=True,
+            )
 
         def add_c(tl, t):
             g, jj = divmod(tl, PACK)
-            nc.vector.tensor_tensor(out=y[:, g, jj, t], in0=tower[tl, t][:], in1=c_all[:, t], op=ALU.add)
-
-        def store_y(tl, t):
-            g, jj = divmod(tl, PACK)
+            if tl in POOL_ADDS:
+                nc.scalar.copy(out=y[:, g, jj, t], in_=tower[tl, t][:])
+                for half in range(2):
+                    o_cols = slice(half * 256, (half + 1) * 256)
+                    nc.gpsimd.tensor_tensor(out=y[:, g, jj, t, o_cols], in0=y[:, g, jj, t, o_cols], in1=c_all[:, t, o_cols], op=ALU.add)
+            else:
+                nc.vector.tensor_tensor(out=y[:, g, jj, t], in0=tower[tl, t][:], in1=c_all[:, t], op=ALU.add)
             nc.sync.dma_start(out=out_view[:, g, jj, t], in_=y[:, g, jj, t])
 
-        def interleave_y(g, t, o0, o1, on_vector):
+        def interleave_y(g, t, o0, o1, engine):
             if (g, t) not in y_k:
                 y_k[g, t] = work.tile([P, O, PACK], BF16, name="y_k", bufs=2, align_bytes=64)
             src = y[:, g, :, t, o0:o1].rearrange("p j o -> p o j")
-            if on_vector:
+            if engine == "vector":
                 nc.vector.tensor_copy(out=y_k[g, t][:, o0:o1], in_=src)
-            else:
+            elif engine == "scalar":
                 nc.scalar.copy(out=y_k[g, t][:, o0:o1], in_=src)
+            else:
+                copy_on_pool(y_k[g, t][:, o0:o1], src)
 
         def quantize_y(g, t):
             m_cols = slice(t * O, (t + 1) * O)
@@ -363,7 +309,6 @@ def tile_mmoetaskgatedexperttowers_x1_kernel(tc, x, we, be, wg, s, wt, c, out_0,
         nc.sync.dma_start(out=wg_sb[:].rearrange("p t j e -> p t (j e)"), in_=wg.rearrange("t (p j) e -> p t (j e)", j=PACK))
         nc.sync.dma_start(out=rows[0:4, :], in_=be)
         nc.sync.dma_start(out=rows[4:6, :], in_=s)
-        nc.sync.dma_start(out=rows[8:12, :].rearrange("c (e f) -> c e f", e=E), in_=be.rearrange("e (c f) -> c e f", c=4))
         for e in range(E):
             load_we(e)
         for ch in range(1, CHUNKS):
@@ -374,59 +319,54 @@ def tile_mmoetaskgatedexperttowers_x1_kernel(tc, x, we, be, wg, s, wt, c, out_0,
             out=c_all[:].rearrange("p t o -> p (t o)"), in_=c.rearrange("t o -> (t o)").partition_broadcast(P)
         )
         make_identity(nc, ident[:])
-        nc.vector.tensor_copy(out=ident_bf[:], in_=ident[:])
-        nc.vector.tensor_reduce(out=diag[:], in_=ident[:].rearrange("p (a i) -> p i a", a=4), axis=AX.X, op=ALU.add)
-        nc.scalar.activation(
-            out=spread[:],
-            in_=ident[:].rearrange("p (a i) -> p a i", a=4).unsqueeze(2).to_broadcast([P, 4, E, GROUP]),
-            func=ACT.Copy,
-        )
+        nc.scalar.activation(out=ident_bf[:], in_=ident[:], func=ACT.Copy)
 
         turn_x(0)
         copy_x(0)
-        col_bank = psum.tile([P, PACK, P], BF16, tag="turn", name="col_bank", bufs=TURN_BANKS)
+        spread_bias(0)
+        logits(0, 2)
+        for j in range(PACK):
+            interleave_we(0, j)
+        quantize_x(0)
+        quantize_we(0)
+        for step in range(5):
+            softmax(0, step)
+            if step != 2:
+                interleave_we(1, step - (step > 2))
+        spread_bias(1)
+        col_bank = psum.tile([P, PACK, P], BF16, tag="spare", name="col_bank", bufs=1)
         for j in range(PACK):
             nc.tensor.transpose(col_bank[:, j], rows[:].rearrange("p (m j) -> p j m", j=PACK)[:, j], ident_bf[:])
+        nc.scalar.copy(out=s_cols[:], in_=col_bank[:, :, 4:6].rearrange("p j t -> p t j"))
 
-        def warm():
-            bank = psum.tile([P, CHUNK_TOK], F32, tag="mix", name="warm_bank")
-            for i in range(WARM):
-                nc.tensor.matmul_mx(
-                    out=bank[:],
-                    lhsT=x_codes[:, :P].bitcast(FP8X4),
-                    lhsT_scale=x_scales[:, :P],
-                    rhs=x_codes[:, :CHUNK_TOK].bitcast(FP8X4),
-                    rhs_scale=x_scales[:, :CHUNK_TOK],
-                    start=True,
-                    stop=True,
-                )
+        order = [(tl, e) for e in range(E) for tl in range(EARLY)] + [(tl, e) for tl in range(EARLY, TILES) for e in range(E)]
+        gates = [(tl, e, t) for tl, e in order[: E * TM_FROM] for t in range(T)]
+        gates += [(tl, e, t) for tl in range(TM_FROM, TILES) for t in range(T) for e in range(E)]
+        sums = {max(FIRST_SUM + SUM_STEP * k, SUM_AT + 2 * k): divmod(k, T) for k in range(TILES * T)}
+        bias_at = [n + BIAS_LAG - (LEAD if n >= E * TM_FROM else 0) for n in range(32)]
 
-        logits(0, 2)
-        for e in range(E):
-            for j in range(PACK):
-                interleave_we(e, j)
-                step = 3 * e + j - SM_AT
-                if j < 3 and 0 <= step < 6:
-                    softmax(0, step)
-                if e == 3 and j > 0:
-                    quantize_we(j - 1)
-            if e == 1:
-                quantize_x(0)
-                nc.scalar.copy(out=cols[:], in_=col_bank[:, :, 0:16])
-                nc.scalar.copy(out=s_cols[:], in_=col_bank[:, :, 4:6].rearrange("p j t -> p t j"))
-                warm()
-        quantize_we(3)
-
-        for n in range(56):
-            if n < 32 and n % RUN == 0:
-                for u in range(n, n + RUN):
-                    experts(u)
-            if n == G1_AT:
-                spread_gates(0)
-            if n == G1_AT + 1:
-                pick_gates(0)
-                diagonal_gates(0)
-                diagonal_gates(1)
+        for n in range(-2, 60):
+            for u in range(32):
+                if bias_at[u] - BIAS_LAG == n:
+                    expert(*order[u])
+            if n - SCALE_LAG - QUANT_LAG - TOWER_LAG in sums:
+                towers(*sums[n - SCALE_LAG - QUANT_LAG - TOWER_LAG])
+            if n in sums:
+                sum_experts(*sums[n])
+            e, k = divmod(n + IL_SHIFT, EARLY)
+            if 1 < e + 1 < E and k == 0:
+                for j in range(PACK):
+                    interleave_we(e + 1, j)
+            for u in range(32):
+                if bias_at[u] == n:
+                    add_bias(*order[u])
+            if n == 1:
+                softmax(0, 5)
+            if n % EARLY == EARLY - 1 and 0 < n // EARLY + 1 < E:
+                quantize_we(n // EARLY + 1)
+            if 0 <= n - GATE_LAG < 32:
+                for t in range(T):
+                    apply_gate(*gates[2 * (n - GATE_LAG) + t])
             for ch in range(1, CHUNKS):
                 if n == X_AT[ch] - 1:
                     turn_x(ch)
@@ -434,61 +374,40 @@ def tile_mmoetaskgatedexperttowers_x1_kernel(tc, x, we, be, wg, s, wt, c, out_0,
                     copy_x(ch)
                 if n == X_AT[ch] + 1:
                     quantize_x(ch)
+            if n == X_AT[1] + 1:
+                logits(2, 4)
+            if 0 <= n - X_AT[1] - 2 < 6:
+                softmax(2, n - X_AT[1] - 2)
             if n == X_AT[3] + 1:
-                logits(2, TILES)
-            for step in range(6):
-                if n == G2_AT + (0, 0, 1, 1, 2, 2)[step]:
-                    softmax(2, step)
-            if n == G2_AT + 3:
-                spread_gates(2)
-                pick_gates(2)
-            if 2 <= n - G2_AT - 1 < TILES:
-                diagonal_gates(n - G2_AT - 1)
-            if 0 <= n - PWT_AT < 4 * PWT_STEP and (n - PWT_AT) % PWT_STEP == 0:
-                interleave_wt(*divmod((n - PWT_AT) // PWT_STEP, 2))
-            tl, k = divmod(n - MIX_LAG - TOWER_LAG, 4)
-            if 0 <= tl < TILES and k == 0:
-                towers(tl)
-            q = n - MIX_LAG
-            if 0 <= q < 32 and q % RUN == 0:
-                for i in range(RUN):
-                    mix(q + i)
-            for back in range(SPAN):
-                for tl, j in finished(n - TURN_LAG - back)[back : back + 1]:
-                    if j in PE_SLOTS:
-                        turn_pe(tl, j)
-                for tl, j in finished(n - TURN_LAG - 1 - back)[back : back + 1]:
-                    if j in PE_SLOTS:
-                        copy_turned(tl, j)
-            if n in (WT_AT, WT_AT + 2):
-                quantize_wt((n - WT_AT) // 2)
-            b, k = divmod(n - MIX_LAG - SCALE_LAG, 2)
-            if 0 <= b < 16 and k == 0:
-                scale_mix(b)
-            for back in range(SPAN):
-                for tl, j in finished(n - TURN_LAG - back)[back : back + 1]:
-                    if j not in PE_SLOTS:
-                        turn_dve(tl, j)
-            tl, k = divmod(n - MIX_LAG - QUANT_LAG, 4)
-            if 0 <= tl < TILES and k == 0:
-                quantize_fs(tl)
-            tl, k = divmod(n - MIX_LAG - ADD_LAG, 4)
-            if 0 <= tl < TILES and k < T:
-                add_c(tl, k)
-                store_y(tl, k)
+                logits(4, TILES)
+            if 0 <= n - G2_AT < 6:
+                softmax(4, n - G2_AT)
+            if 0 <= n - WT_AT < 4:
+                for part in range(2):
+                    interleave_wt(*divmod(2 * (n - WT_AT) + part, 4))
+            if n in (WTQ_AT, WTQ_AT + 2):
+                quantize_wt((n - WTQ_AT) // 2)
+            if n - SCALE_LAG in sums:
+                scale_mix(*sums[n - SCALE_LAG])
+            if n - SCALE_LAG - QUANT_LAG in sums:
+                quantize_fs(*sums[n - SCALE_LAG - QUANT_LAG])
+            last = n - SCALE_LAG - QUANT_LAG - TOWER_LAG - ADD_LAG
+            if last in sums:
+                add_c(*sums[last])
             piece = n - Y0_AT
-            if 0 <= piece < 4:
-                interleave_y(0, piece // 2, 256 * (piece % 2), 256 * (piece % 2 + 1), on_vector=False)
-            if n in (Y0_AT + 3, Y0_AT + 5):
-                quantize_y(0, (n - Y0_AT - 3) // 2)
-            if n == Y0_AT + 5:
+            if 0 <= piece < 8:
+                interleave_y(0, piece // 4, P * (piece % 4), P * (piece % 4 + 1), "pool")
+            if piece in (Y0Q, Y0Q + 4):
+                quantize_y(0, piece // (Y0Q + 4))
+            if piece == Y0Q + 4:
                 store_scales(0)
-            t = n - (MIX_LAG + ADD_LAG + 28)
-            if 0 <= t < T:
-                interleave_y(1, t, 0, Y_CUT, on_vector=False)
-            if t == 1:
-                interleave_y(1, 0, Y_CUT, O, on_vector=True)
-                interleave_y(1, 1, Y_CUT, O, on_vector=True)
-                quantize_y(1, 0)
-                quantize_y(1, 1)
-                store_scales(1)
+            if last in sums and sums[last][0] == TILES - 1:
+                t = sums[last][1]
+                cut = (Y_CUT0, Y_CUT)[t]
+                interleave_y(1, t, 0, cut, "scalar")
+                if cut < O:
+                    interleave_y(1, t, cut, O, "vector")
+                if t == 1:
+                    quantize_y(1, 0)
+                    quantize_y(1, 1)
+                    store_scales(1)

from contextlib import ExitStack

import concourse.mybir as mybir
from concourse.masks import make_identity

N_TOK, D, E, F, T, O = 1024, 512, 4, 512, 2, 512
FLOPS = 2 * N_TOK * D * E * F + 2 * N_TOK * D * T * E + 2 * T * N_TOK * F * O

F32 = mybir.dt.float32
BF16 = mybir.dt.bfloat16
I32 = mybir.dt.int32
U32 = mybir.dt.uint32
U8 = mybir.dt.uint8
FP8X4 = mybir.dt.float8_e4m3fn_x4
ACT = mybir.ActivationFunctionType
ALU = mybir.AluOpType
AX = mybir.AxisListType

P = 128
PACK = 4
TILES = 8
CHUNKS = 4
WE_CUT = 3
WE_CUT0 = 4
POOL_ADDS = ()
EARLY = 2
BIAS_LAG = 1
GATE_LAG = 2
FIRST_SUM = 9
SUM_STEP = 1
SUM_AT = 9
SCALE_LAG = 1
QUANT_LAG = 1
TOWER_LAG = 1
ADD_LAG = 1
X_AT = (0, 2, 4, 6)
G2_AT = 8
WT_AT = 4
WTQ_AT = 9
Y0_AT = 28
Y0Q = 6
Y_CUT0 = 256
TM_FROM = 8
LEAD = 0
IL_SHIFT = 0
Y_CUT = 192
DVE_GATES = ()
EXPERT_BANKS = 3
ZB_BUFS = 8
U_BUFS = 22
WARM = 0


def tile_mmoetaskgatedexperttowers_x1_kernel(tc, x, we, be, wg, s, wt, c, out_0, out_1, out_2):
    nc = tc.nc
    with ExitStack() as ctx:
        keep = ctx.enter_context(tc.tile_pool(name="keep", bufs=1))
        work = ctx.enter_context(tc.tile_pool(name="work", bufs=2))
        psum = ctx.enter_context(tc.psum_pool(name="psum", bufs=2))
        ctx.enter_context(tc.manual_schedule())

        ident = keep.tile([P, P], F32, align_bytes=64)
        ident_bf = keep.tile([P, P], BF16, align_bytes=64)
        rows = keep.tile([P, F], BF16)
        s_cols = keep.tile([P, T, PACK], F32)
        wg_sb = keep.tile([P, T, PACK, E], BF16)
        be_all = keep.tile([P, E, F], BF16, align_bytes=64)
        c_all = keep.tile([P, T, O], BF16, align_bytes=64)
        x_raw = keep.tile([P, CHUNKS, 2, D], BF16, align_bytes=64)
        x_k = keep.tile([P, N_TOK * PACK], BF16, align_bytes=64)
        x_codes = keep.tile([P, N_TOK], U32, align_bytes=64)
        x_scales = keep.tile([P, N_TOK], U8, align_bytes=64)
        we_raw = keep.tile([P, E, PACK, F], BF16, align_bytes=64)
        we_k = keep.tile([P, E, PACK, P, PACK], BF16, align_bytes=64)
        we_codes = keep.tile([P, E, F], U32, align_bytes=64)
        we_scales = keep.tile([P, E, F], U8, align_bytes=64)
        wt_raw = keep.tile([P, T, PACK, O], BF16, align_bytes=64)
        wt_k = keep.tile([P, T, O, PACK], BF16, align_bytes=64)
        wt_codes = keep.tile([P, T, O], U32, align_bytes=64)
        wt_scales = keep.tile([P, T, O], U8, align_bytes=64)
        gate = keep.tile([P, TILES * T, E], F32)
        y = keep.tile([P, 2, PACK, T, O], F32, align_bytes=64)
        y_codes = keep.tile([P, 2, T * O], U32, align_bytes=64)
        y_scales = keep.tile([P, 2, T * O], U8, align_bytes=64)

        expert_bank, pre, gated, mix_bank, fs_k, fs_q, tower, y_k, x_bank, gate_state = ({} for i in range(10))

        x_view = x.rearrange("(g m j) d -> m g j d", g=2, j=PACK)
        out_view = out_0.rearrange("t (g m j) o -> m g j t o", g=2, j=PACK)
        words_view = out_1.rearrange("g p m b -> p g (m b)").bitcast(I32)

        def load_x(ch):
            g, j0 = divmod(2 * ch, PACK)
            nc.sync.dma_start(out=x_raw[:, ch], in_=x_view[:, g, j0 : j0 + 2, :])

        def load_we(e):
            nc.sync.dma_start(out=we_raw[:, e], in_=we[e].rearrange("(p j) f -> p j f", j=PACK))

        def load_wt(t):
            nc.sync.dma_start(out=wt_raw[:, t], in_=wt[t].rearrange("(p j) o -> p j o", j=PACK))

        def turn_x(ch):
            bank = psum.tile([P, 2, 2, P], F32, tag="spare", name="x_bank", bufs=1)
            x_bank[ch] = bank
            for tl in range(2):
                words = x_raw[:, ch, tl, :].bitcast(F32).rearrange("p (w u) -> p u w", u=2)
                for u in range(2):
                    nc.tensor.transpose(bank[:, tl, u, :], words[:, u, :], ident[:])

        def copy_x(ch):
            dst = x_k[:, ch * 1024 : (ch + 1) * 1024].bitcast(F32).rearrange("p (t m u) -> p t m u", t=2, u=2)
            nc.scalar.copy(out=dst, in_=x_bank[ch][:].rearrange("p t u m -> p t m u"))

        def quantize_x(ch):
            tok = slice(ch * 2 * P, (ch + 1) * 2 * P)
            nc.vector.quantize_mx(
                out=x_codes[:, tok].bitcast(FP8X4), scales=x_scales[:, tok], in_=x_k[:, ch * 1024 : (ch + 1) * 1024]
            )

        def logits(t0, t1):
            n = t1 - t0
            q = psum.tile([P, n, T, E], F32, tag="tower", name="logits")
            x_cols = x_k[:].rearrange("p (n j) -> p j n", j=PACK)
            for tl in range(n):
                for j in range(PACK):
                    nc.tensor.matmul(
                        q[:, tl],
                        lhsT=x_cols[:, j, (t0 + tl) * P : (t0 + tl + 1) * P],
                        rhs=wg_sb[:, :, j, :],
                        start=(j == 0),
                        stop=(j == PACK - 1),
                    )
            top = work.tile([P, n * T], F32, name="top")
            den = work.tile([P, n * T], F32, name="den")
            gate_state[t0] = (n, q[:].rearrange("p n t e -> p (n t) e"), top, den)

        def softmax(t0, step):
            n, q, top, den = gate_state[t0]
            num = gate[:, t0 * T : (t0 + n) * T]
            full = [P, n * T, E]
            if step == 0:
                nc.vector.tensor_reduce(out=top[:], in_=q, axis=AX.X, op=ALU.max)
            elif step == 1:
                nc.vector.tensor_tensor(out=num, in0=q, in1=top[:].unsqueeze(2).to_broadcast(full), op=ALU.subtract)
            elif step == 2:
                nc.scalar.activation(out=num, in_=num, func=ACT.Exp)
            elif step == 3:
                nc.vector.tensor_reduce(out=den[:], in_=num, axis=AX.X, op=ALU.add)
            elif step == 4:
                nc.vector.reciprocal(out=den[:], in_=den[:])
            else:
                nc.vector.tensor_tensor(out=num, in0=num, in1=den[:].unsqueeze(2).to_broadcast(full), op=ALU.mult)

        def spread_bias(half):
            bank = psum.tile([P, 2, F], BF16, tag="mix", name="bias_bank")
            for i in range(2):
                e = 2 * half + i
                nc.tensor.matmul(
                    bank[:, i].rearrange("p (j m) -> p j m", j=PACK),
                    lhsT=ident_bf[:, e : e + 1].to_broadcast([P, P]),
                    rhs=rows[:].rearrange("p (m j) -> p j m", j=PACK),
                    start=True,
                    stop=True,
                )
            nc.scalar.copy(out=be_all[:, 2 * half : 2 * half + 2], in_=bank[:])

        def interleave_we(e, j):
            src = we_raw[:, e].rearrange("p d (m j) -> p j m d", j=PACK)[:, j]
            if j >= (WE_CUT if e > 0 else WE_CUT0):
                nc.scalar.copy(out=we_k[:, e, j], in_=src)
            else:
                nc.vector.tensor_copy(out=we_k[:, e, j], in_=src)

        def quantize_we(e):
            nc.vector.quantize_mx(
                out=we_codes[:, e].bitcast(FP8X4),
                scales=we_scales[:, e],
                in_=we_k[:, e].rearrange("p j m d -> p (j m d)"),
            )

        def copy_on_pool(dst, src):
            nc.gpsimd.tensor_scalar(out=dst, in0=src, scalar1=1.0, scalar2=0.0, op0=ALU.mult, op1=ALU.add)

        def interleave_wt(t, part):
            o_cols = slice(part * P, (part + 1) * P)
            copy_on_pool(wt_k[:, t, o_cols, :], wt_raw[:, t, :, o_cols].rearrange("p d o -> p o d"))

        def quantize_wt(t):
            nc.vector.quantize_mx(
                out=wt_codes[:, t].bitcast(FP8X4),
                scales=wt_scales[:, t],
                in_=wt_k[:, t].rearrange("p o d -> p (o d)"),
            )

        def expert(tl, e):
            tok = slice(tl * P, (tl + 1) * P)
            bank = psum.tile([P, F], F32, tag="expert", name="expert_bank", bufs=EXPERT_BANKS)
            expert_bank[tl, e] = bank
            nc.tensor.matmul_mx(
                out=bank[:],
                lhsT=x_codes[:, tok].bitcast(FP8X4),
                lhsT_scale=x_scales[:, tok],
                rhs=we_codes[:, e].bitcast(FP8X4),
                rhs_scale=we_scales[:, e],
                start=True,
                stop=True,
            )

        def add_bias(tl, e):
            pre[tl, e] = work.tile([P, F], F32, name="pre", bufs=ZB_BUFS, align_bytes=64)
            nc.vector.tensor_tensor(out=pre[tl, e][:], in0=expert_bank[tl, e][:], in1=be_all[:, e], op=ALU.add)

        def apply_gate(tl, e, t):
            gated[tl, e, t] = work.tile([P, PACK, P], F32, name="gated", bufs=U_BUFS, align_bytes=64)
            dst = gated[tl, e, t][:].rearrange("p j m -> p (j m)")
            g = gate[:, tl * T + t, e : e + 1]
            if (e, t) in DVE_GATES:
                nc.vector.tensor_scalar(out=dst, in0=pre[tl, e][:], scalar1=g, scalar2=0.0, op0=ALU.mult, op1=ALU.max)
            else:
                nc.scalar.activation(out=dst, in_=pre[tl, e][:], func=ACT.Relu, scale=g)

        def sum_experts(tl, t):
            bank = psum.tile([P, PACK, P], F32, tag="mix", name="mix_bank")
            mix_bank[tl, t] = bank
            for j in range(PACK):
                for e in range(E):
                    nc.tensor.matmul(
                        bank[:, j],
                        lhsT=gated[tl, e, t][:, j],
                        rhs=ident[:],
                        start=(e == 0),
                        stop=(e == E - 1),
                        is_transpose=True,
                    )

        def scale_mix(tl, t):
            if t == 0:
                fs_k[tl] = work.tile([P, T, P, PACK], BF16, name="fs_k", bufs=2, align_bytes=64)
            nc.vector.tensor_tensor(
                out=fs_k[tl][:, t],
                in0=mix_bank[tl, t][:].rearrange("p j n -> p n j"),
                in1=s_cols[:, t].unsqueeze(1).to_broadcast([P, P, PACK]),
                op=ALU.mult,
            )

        def quantize_fs(tl, t):
            codes = work.tile([P, P], U32, name="fs_codes", bufs=3, align_bytes=64)
            scales = work.tile([P, P], U8, name="fs_scales", bufs=3, align_bytes=64)
            fs_q[tl, t] = (codes, scales)
            nc.vector.quantize_mx(
                out=codes[:].bitcast(FP8X4), scales=scales[:], in_=fs_k[tl][:, t].rearrange("p m j -> p (m j)")
            )

        def towers(tl, t):
            codes, scales = fs_q[tl, t]
            bank = psum.tile([P, O], F32, tag="tower", name="tower_bank")
            tower[tl, t] = bank
            nc.tensor.matmul_mx(
                out=bank[:],
                lhsT=codes[:].bitcast(FP8X4),
                lhsT_scale=scales[:],
                rhs=wt_codes[:, t].bitcast(FP8X4),
                rhs_scale=wt_scales[:, t],
                start=True,
                stop=True,
            )

        def add_c(tl, t):
            g, jj = divmod(tl, PACK)
            if tl in POOL_ADDS:
                nc.scalar.copy(out=y[:, g, jj, t], in_=tower[tl, t][:])
                for half in range(2):
                    o_cols = slice(half * 256, (half + 1) * 256)
                    nc.gpsimd.tensor_tensor(out=y[:, g, jj, t, o_cols], in0=y[:, g, jj, t, o_cols], in1=c_all[:, t, o_cols], op=ALU.add)
            else:
                nc.vector.tensor_tensor(out=y[:, g, jj, t], in0=tower[tl, t][:], in1=c_all[:, t], op=ALU.add)
            nc.sync.dma_start(out=out_view[:, g, jj, t], in_=y[:, g, jj, t])

        def interleave_y(g, t, o0, o1, engine):
            if (g, t) not in y_k:
                y_k[g, t] = work.tile([P, O, PACK], BF16, name="y_k", bufs=2, align_bytes=64)
            src = y[:, g, :, t, o0:o1].rearrange("p j o -> p o j")
            if engine == "vector":
                nc.vector.tensor_copy(out=y_k[g, t][:, o0:o1], in_=src)
            elif engine == "scalar":
                nc.scalar.copy(out=y_k[g, t][:, o0:o1], in_=src)
            else:
                copy_on_pool(y_k[g, t][:, o0:o1], src)

        def quantize_y(g, t):
            m_cols = slice(t * O, (t + 1) * O)
            nc.vector.quantize_mx(
                out=y_codes[:, g, m_cols].bitcast(FP8X4),
                scales=y_scales[:, g, m_cols],
                in_=y_k[g, t][:].rearrange("p o j -> p (o j)"),
            )
            nc.sync.dma_start(out=words_view[:, g, m_cols], in_=y_codes[:, g, m_cols].bitcast(I32))

        def store_scales(g):
            for quad in range(4):
                eng = nc.scalar if g == 1 and quad % 2 else nc.sync
                eng.dma_start(
                    out=out_2[g, 4 * quad : 4 * quad + 4, :].bitcast(I32),
                    in_=y_scales[32 * quad : 32 * quad + 4, g].bitcast(I32),
                )

        nc.vector.memset(rows[:], 0.0)
        load_x(0)
        nc.sync.dma_start(out=wg_sb[:].rearrange("p t j e -> p t (j e)"), in_=wg.rearrange("t (p j) e -> p t (j e)", j=PACK))
        nc.sync.dma_start(out=rows[0:4, :], in_=be)
        nc.sync.dma_start(out=rows[4:6, :], in_=s)
        for e in range(E):
            load_we(e)
        for ch in range(1, CHUNKS):
            load_x(ch)
        for t in range(T):
            load_wt(t)
        nc.sync.dma_start(
            out=c_all[:].rearrange("p t o -> p (t o)"), in_=c.rearrange("t o -> (t o)").partition_broadcast(P)
        )
        make_identity(nc, ident[:])
        nc.scalar.activation(out=ident_bf[:], in_=ident[:], func=ACT.Copy)

        turn_x(0)
        copy_x(0)
        spread_bias(0)
        logits(0, 2)
        for j in range(PACK):
            interleave_we(0, j)
        quantize_x(0)
        quantize_we(0)
        for step in range(5):
            softmax(0, step)
            if step != 2:
                interleave_we(1, step - (step > 2))
        spread_bias(1)
        col_bank = psum.tile([P, PACK, P], BF16, tag="spare", name="col_bank", bufs=1)
        for j in range(PACK):
            nc.tensor.transpose(col_bank[:, j], rows[:].rearrange("p (m j) -> p j m", j=PACK)[:, j], ident_bf[:])
        nc.scalar.copy(out=s_cols[:], in_=col_bank[:, :, 4:6].rearrange("p j t -> p t j"))

        order = [(tl, e) for e in range(E) for tl in range(EARLY)] + [(tl, e) for tl in range(EARLY, TILES) for e in range(E)]
        gates = [(tl, e, t) for tl, e in order[: E * TM_FROM] for t in range(T)]
        gates += [(tl, e, t) for tl in range(TM_FROM, TILES) for t in range(T) for e in range(E)]
        sums = {max(FIRST_SUM + SUM_STEP * k, SUM_AT + 2 * k): divmod(k, T) for k in range(TILES * T)}
        bias_at = [n + BIAS_LAG - (LEAD if n >= E * TM_FROM else 0) for n in range(32)]

        for n in range(-2, 60):
            for u in range(32):
                if bias_at[u] - BIAS_LAG == n:
                    expert(*order[u])
            if n - SCALE_LAG - QUANT_LAG - TOWER_LAG in sums:
                towers(*sums[n - SCALE_LAG - QUANT_LAG - TOWER_LAG])
            if n in sums:
                sum_experts(*sums[n])
            e, k = divmod(n + IL_SHIFT, EARLY)
            if 1 < e + 1 < E and k == 0:
                for j in range(PACK):
                    interleave_we(e + 1, j)
            for u in range(32):
                if bias_at[u] == n:
                    add_bias(*order[u])
            if n == 1:
                softmax(0, 5)
            if n % EARLY == EARLY - 1 and 0 < n // EARLY + 1 < E:
                quantize_we(n // EARLY + 1)
            if 0 <= n - GATE_LAG < 32:
                for t in range(T):
                    apply_gate(*gates[2 * (n - GATE_LAG) + t])
            for ch in range(1, CHUNKS):
                if n == X_AT[ch] - 1:
                    turn_x(ch)
                if n == X_AT[ch]:
                    copy_x(ch)
                if n == X_AT[ch] + 1:
                    quantize_x(ch)
            if n == X_AT[1] + 1:
                logits(2, 4)
            if 0 <= n - X_AT[1] - 2 < 6:
                softmax(2, n - X_AT[1] - 2)
            if n == X_AT[3] + 1:
                logits(4, TILES)
            if 0 <= n - G2_AT < 6:
                softmax(4, n - G2_AT)
            if 0 <= n - WT_AT < 4:
                for part in range(2):
                    interleave_wt(*divmod(2 * (n - WT_AT) + part, 4))
            if n in (WTQ_AT, WTQ_AT + 2):
                quantize_wt((n - WTQ_AT) // 2)
            if n - SCALE_LAG in sums:
                scale_mix(*sums[n - SCALE_LAG])
            if n - SCALE_LAG - QUANT_LAG in sums:
                quantize_fs(*sums[n - SCALE_LAG - QUANT_LAG])
            last = n - SCALE_LAG - QUANT_LAG - TOWER_LAG - ADD_LAG
            if last in sums:
                add_c(*sums[last])
            piece = n - Y0_AT
            if 0 <= piece < 8:
                interleave_y(0, piece // 4, P * (piece % 4), P * (piece % 4 + 1), "pool")
            if piece in (Y0Q, Y0Q + 4):
                quantize_y(0, piece // (Y0Q + 4))
            if piece == Y0Q + 4:
                store_scales(0)
            if last in sums and sums[last][0] == TILES - 1:
                t = sums[last][1]
                cut = (Y_CUT0, Y_CUT)[t]
                interleave_y(1, t, 0, cut, "scalar")
                if cut < O:
                    interleave_y(1, t, cut, O, "vector")
                if t == 1:
                    quantize_y(1, 0)
                    quantize_y(1, 1)
                    store_scales(1)
